import numpy as np, ml_dtypes
CORES = [24,26,29,31,48,50,53,55]
N = 8
import mx_ref
NC = 384
SEQ = [0,0,0,1,1,1,2,2]
WID = [384,226,134,256,178,202,368,128]
BF = ml_dtypes.bfloat16
def setup_inputs(rng):
    def f(*shape):
        return mx_ref.flush((rng.standard_normal(shape, dtype=np.float32) * np.exp2(rng.integers(-2, 3, shape[:-1] + (1,)))).astype(BF))
    return {"w": f(N, 128, 512), "x": f(N, 128, 4 * NC)}
def setup_inputs_blocks(rng):
    d = setup_inputs(rng)
    for k in ("w", "x"): d[k] = mx_ref.spread(d[k], rng, 4)
    return d
def setup_inputs_wide(rng):
    d = setup_inputs(rng)
    for k in ("w", "x"): d[k] = mx_ref.flush((d[k].astype(np.float32) * np.exp2(rng.integers(-10, 11, (N, 1, 1))).astype(np.float32)).astype(BF))
    return d
def reference(w, x):
    y = np.full((N, 128, 744), np.nan, np.float32)
    for r in range(N):
        qw = mx_ref.quantize(w[r]); a = 0
        for j in range(N):
            if SEQ[j] == SEQ[r]:
                y[r][:, a:a + WID[j]] = mx_ref.matmul(qw, mx_ref.quantize(x[j][:, :4 * WID[j]])); a += WID[j]
    return {"y": y}

@@ -1,0 +1,176 @@
+from concourse.bass import DstId, RemoteDMATransfer
+from concourse.mybir import dt
+
+N = 8
+NC = 384
+YC = 744
+MAXB = 3
+
+SCRATCH = {
+    "xb": ("sbuf", [128, 4 * NC], "bfloat16"),
+    "wb": ("sbuf", [128, 512], "bfloat16"),
+    "qw": ("sbuf", [128, 128], "float8_e4m3fn_x4"),
+    "pw": ("sbuf", [128, 128], "uint8"),
+    "ps": ("psum", [128, 512 * MAXB], "float32"),
+    "yo": ("sbuf", [128, YC], "float32"),
+}
+SCRATCH.update({"q%d" % j: ("sbuf", [128, NC], "float8_e4m3fn_x4") for j in range(N)})
+SCRATCH.update({"p%d" % j: ("sbuf", [128, NC], "uint8") for j in range(N)})
+
+SEMAPHORES = (["xl", "wl", "qx", "qwd", "st", "sent"]
+              + ["ac%d" % j for j in range(N)] + ["ap%d" % j for j in range(N)]
+              + ["mm%d" % k for k in range(MAXB)] + ["cp%d" % k for k in range(MAXB)])
+
+
+def _bits(mask):
+    return [1 << b for b in range(mask.bit_length()) if (mask >> b) & 1]
+
+
+def _join(bits):
+    m = 0
+    for b in bits:
+        m |= b
+    return m
+
+
+def _routes(T, topo):
+    cores = list(T.cores)
+    seq = T.tables["SEQ"]
+    own = {c: [] for c in cores}
+    fwd = {c: [] for c in cores}
+    for j, o in enumerate(cores):
+        readers = [cores[d] for d in range(N) if seq[d] == seq[j] and d != j]
+        near = [d for d in readers if topo.chip(d) == topo.chip(o)]
+        far = [d for d in readers if topo.chip(d) != topo.chip(o)]
+        handed = False
+        for ch in sorted({topo.chip(d) for d in far}):
+            grp = [d for d in far if topo.chip(d) == ch]
+            entry, rest = grp[0], grp[1:]
+            if topo.may_write(o, entry):
+                own[o].append((j, "c", [[entry]]))
+                own[o].append((j, "p", [grp]))
+            else:
+                handed = True
+                gates = [c for c in cores if c != o and topo.chip(c) == topo.chip(o) and topo.may_write(c, entry)]
+                gate_p = ([c for c in gates if c in near] + gates)[0]
+                gate_c = ([c for c in gates if c not in near] + gates)[0]
+                if gate_c not in near:
+                    own[o].append((j, "c", [[gate_c]]))
+                if gate_p not in near:
+                    own[o].append((j, "p", [[gate_p]]))
+                fwd[gate_c].append((j, "c", [[entry]]))
+                fwd[gate_p].append((j, "p", [grp]))
+            if rest:
+                fwd[entry].append((j, "c", [rest]))
+        if near:
+            legs = [[d] for d in sorted(near, key=lambda d: topo.die(d) == topo.die(o))]
+            for part in ("p", "c") if handed else ("c", "p"):
+                own[o].append((j, part, legs))
+    return own, fwd
+
+
+def _masks(topo, core, own, fwd):
+    def leaves(call):
+        return any(topo.chip(d) != topo.chip(core) for leg in call[2] for d in leg)
+    away = [d for call in own + fwd for leg in call[2] for d in leg if topo.chip(d) != topo.chip(core)]
+    off = topo.mask(core, away[0]) if away else 0
+    own_leaves = any(leaves(call) for call in own)
+
+    def with_masks(call):
+        tile, part, legs = call
+        if leaves(call):
+            return tile, part, [(topo.mask(core, leg[0]), leg) for leg in legs]
+        full = topo.mask(core, legs[0][0])
+        if off and own_leaves:
+            pool = _bits(full & ~off)
+        elif off:
+            pool = _bits(full & off)
+        elif len(legs) == 1:
+            pool = _bits(full)[0::2]
+        else:
+            pool = _bits(full)
+        return tile, part, [(_join(pool[k::len(legs)]), leg) for k, leg in enumerate(legs)]
+    return [with_masks(c) for c in own], [with_masks(c) for c in fwd]
+
+
+def _piece(T, tile, part, n):
+    if part == "c":
+        return T["q%d" % tile][:, 0:n].bitcast(dt.uint8)
+    return T["p%d" % tile][:, 0:n]
+
+
+def _send(g, T, topo, call):
+    tile, part, legs = call
+    n = T.tables["WID"][tile]
+    sem = T.sem["a%s%d" % (part, tile)]
+    if len(legs) == 1 and len(legs[0][1]) == 1:
+        mask, (dst,) = legs[0]
+        rid, pid, _ = topo.addr(dst)
+        g.remote_dma(out_ap=_piece(T, tile, part, n), in_ap=_piece(T, tile, part, n), remote_sem=sem,
+                     local_sem=T.sem.sent, pid=pid, routing_id=rid, dma_engine_mask=mask)
+    else:
+        g.remote_dma_fused(
+            [RemoteDMATransfer(dst_ids=[DstId(rid=topo.addr(d)[0], pnc=topo.addr(d)[1]) for d in dsts],
+                               dma_engine_mask=mask, remote_sem=sem,
+                               srcs=[_piece(T, tile, part, n)], dsts=[_piece(T, tile, part, n) for d in dsts])
+             for mask, dsts in legs],
+            local_sem=T.sem.sent)
+    return sum(len(_bits(mask)) for mask, dsts in legs)
+
+
+def rank_program(g, core, T, topo):
+    rank = T.rank_of(core)
+    if rank is None:
+        return
+    cores = list(T.cores)
+    seq, wid = T.tables["SEQ"], T.tables["WID"]
+    own, fwd = _routes(T, topo)
+    calls = {c: _masks(topo, c, own[c], fwd[c]) for c in cores}
+    lands = {}
+    for c in cores:
+        for tile, part, legs in calls[c][0] + calls[c][1]:
+            for mask, dsts in legs:
+                if core in dsts:
+                    lands[(tile, part)] = (len(_bits(mask)), c)
+
+    n = wid[rank]
+    g.sync.dma_start(T.xb[:, 0:4 * n], T.x[:, 0:4 * n]).then_inc(T.sem.xl, 16)
+    g.sync.dma_start(T.wb[:], T.w[:]).then_inc(T.sem.wl, 16)
+    g.vector.wait_ge(T.sem.xl, 16)
+    g.vector.quantize_mx(T["q%d" % rank][:, 0:n], T["p%d" % rank][:, 0:n], T.xb[:, 0:4 * n]).then_inc(T.sem.qx, 1)
+    g.vector.wait_ge(T.sem.wl, 16)
+    g.vector.quantize_mx(T.qw[:], T.pw[:], T.wb[:]).then_inc(T.sem.qwd, 1)
+
+    sent = 0
+    g.wait_ge(T.sem.qx, 1)
+    for call in calls[core][0]:
+        sent += _send(g, T, topo, call)
+    for call in calls[core][1]:
+        g.wait_ge(T.sem["a%s%d" % (call[1], call[0])], lands[(call[0], call[1])][0])
+        sent += _send(g, T, topo, call)
+
+    members = [j for j in range(N) if seq[j] == seq[rank]]
+    col = {j: sum(wid[i] for i in members if i < j) for j in members}
+
+    def expected(j):
+        relayed = any(lands[(j, part)][1] != cores[j] for part in ("c", "p"))
+        return (topo.chip(cores[j]) != topo.chip(core), relayed, wid[j])
+    order = [rank] + sorted((j for j in members if j != rank), key=expected)
+
+    g.tensor.wait_ge(T.sem.qwd, 1)
+    for k, j in enumerate(order):
+        m, a = wid[j], col[j]
+        if j == rank:
+            g.tensor.wait_ge(T.sem.qx, 1)
+        else:
+            g.tensor.wait_ge(T.sem["ac%d" % j], lands[(j, "c")][0])
+            g.tensor.wait_ge(T.sem["ap%d" % j], lands[(j, "p")][0])
+        g.tensor.matmul_mx(T.ps[:, 512 * k:512 * k + m], T.qw[:], T.pw[:], T["q%d" % j][:, 0:m], T["p%d" % j][:, 0:m],
+                           True, True).then_inc(T.sem["mm%d" % k], 1)
+        g.vector.wait_ge(T.sem["mm%d" % k], 1)
+        g.vector.tensor_copy(T.yo[:, a:a + m], T.ps[:, 512 * k:512 * k + m]).then_inc(T.sem["cp%d" % k], 1)
+        g.sync.wait_ge(T.sem["cp%d" % k], 1)
+        g.sync.dma_start(T.y[:, a:a + m], T.yo[:, a:a + m]).then_inc(T.sem.st, 16)
+
+    g.wait_ge(T.sem.sent, sent)
+    g.wait_ge(T.sem.st, 16 * len(order))

@@ -4,7 +4,8 @@ from concourse.mybir import dt
 N = 8
 NC = 384
 YC = 744
-MAXB = 3
+MAXB = 4
+LEAST = 128
 
 SCRATCH = {
     "xb": ("sbuf", [128, 4 * NC], "bfloat16"),
@@ -17,8 +18,8 @@ SCRATCH = {
 SCRATCH.update({"q%d" % j: ("sbuf", [128, NC], "float8_e4m3fn_x4") for j in range(N)})
 SCRATCH.update({"p%d" % j: ("sbuf", [128, NC], "uint8") for j in range(N)})
 
-SEMAPHORES = (["xl", "wl", "qx", "qwd", "st", "sent"]
-              + ["ac%d" % j for j in range(N)] + ["ap%d" % j for j in range(N)]
+SEMAPHORES = (["xl0", "xl1", "wl", "qx0", "qx1", "qwd", "st", "sent"]
+              + ["a%s%d_%d" % (part, j, k) for part in "cp" for j in range(N) for k in range(2)]
               + ["mm%d" % k for k in range(MAXB)] + ["cp%d" % k for k in range(MAXB)])
 
 
@@ -33,7 +34,21 @@ def _join(bits):
     return m
 
 
-def _routes(T, topo):
+def _cuts(T, topo):
+    cores, seq, wid = list(T.cores), T.tables["SEQ"], T.tables["WID"]
+    cuts, whole = [], []
+    for j in range(N):
+        n = wid[j]
+        whole.append(any(seq[d] == seq[j] and topo.chip(cores[d]) != topo.chip(cores[j]) for d in range(N)))
+        if n >= 2 * LEAST:
+            h = n // 4 * 2
+            cuts.append([(0, h), (h, n)])
+        else:
+            cuts.append([(0, n)])
+    return cuts, whole
+
+
+def _routes(T, topo, cuts, whole):
     cores = list(T.cores)
     seq = T.tables["SEQ"]
     own = {c: [] for c in cores}
@@ -42,44 +57,46 @@ def _routes(T, topo):
         readers = [cores[d] for d in range(N) if seq[d] == seq[j] and d != j]
         near = [d for d in readers if topo.chip(d) == topo.chip(o)]
         far = [d for d in readers if topo.chip(d) != topo.chip(o)]
-        handed = False
-        for ch in sorted({topo.chip(d) for d in far}):
-            grp = [d for d in far if topo.chip(d) == ch]
-            entry, rest = grp[0], grp[1:]
-            if topo.may_write(o, entry):
-                own[o].append((j, "c", [[entry]]))
-                own[o].append((j, "p", [grp]))
-            else:
-                handed = True
-                gates = [c for c in cores if c != o and topo.chip(c) == topo.chip(o) and topo.may_write(c, entry)]
-                gate_p = ([c for c in gates if c in near] + gates)[0]
-                gate_c = ([c for c in gates if c not in near] + gates)[0]
-                if gate_c not in near:
-                    own[o].append((j, "c", [[gate_c]]))
-                if gate_p not in near:
-                    own[o].append((j, "p", [[gate_p]]))
-                fwd[gate_c].append((j, "c", [[entry]]))
-                fwd[gate_p].append((j, "p", [grp]))
-            if rest:
-                fwd[entry].append((j, "c", [rest]))
-        if near:
-            legs = [[d] for d in sorted(near, key=lambda d: topo.die(d) == topo.die(o))]
-            for part in ("p", "c") if handed else ("c", "p"):
-                own[o].append((j, part, legs))
+        for k in range(len(cuts[j])):
+            handed = False
+            plane = [] if whole[j] and k + 1 < len(cuts[j]) else [0 if whole[j] else k]
+            for ch in sorted({topo.chip(d) for d in far}):
+                grp = [d for d in far if topo.chip(d) == ch]
+                entry, rest = grp[0], grp[1:]
+                if topo.may_write(o, entry):
+                    own[o].append((j, k, "c", [[entry]]))
+                    own[o] += [(j, kp, "p", [grp]) for kp in plane]
+                else:
+                    handed = True
+                    gates = [c for c in cores if c != o and topo.chip(c) == topo.chip(o) and topo.may_write(c, entry)]
+                    gate_p = ([c for c in gates if c in near] + gates)[0]
+                    gate_c = ([c for c in gates if c not in near] + gates)[0]
+                    if gate_c not in near:
+                        own[o].append((j, k, "c", [[gate_c]]))
+                    if gate_p not in near:
+                        own[o] += [(j, kp, "p", [[gate_p]]) for kp in plane]
+                    fwd[gate_c].append((j, k, "c", [[entry]]))
+                    fwd[gate_p] += [(j, kp, "p", [grp]) for kp in plane]
+                if rest:
+                    fwd[entry].append((j, k, "c", [rest]))
+            if near:
+                legs = [[d] for d in sorted(near, key=lambda d: topo.die(d) == topo.die(o))]
+                for part in ("p", "c") if handed else ("c", "p"):
+                    own[o] += [(j, kk, part, legs) for kk in ([k] if part == "c" else plane)]
     return own, fwd
 
 
 def _masks(topo, core, own, fwd):
     def leaves(call):
-        return any(topo.chip(d) != topo.chip(core) for leg in call[2] for d in leg)
-    away = [d for call in own + fwd for leg in call[2] for d in leg if topo.chip(d) != topo.chip(core)]
+        return any(topo.chip(d) != topo.chip(core) for leg in call[3] for d in leg)
+    away = [d for call in own + fwd for leg in call[3] for d in leg if topo.chip(d) != topo.chip(core)]
     off = topo.mask(core, away[0]) if away else 0
     own_leaves = any(leaves(call) for call in own)
 
     def with_masks(call):
-        tile, part, legs = call
+        tile, run, part, legs = call
         if leaves(call):
-            return tile, part, [(topo.mask(core, leg[0]), leg) for leg in legs]
+            return tile, run, part, [(topo.mask(core, leg[0]), leg) for leg in legs]
         full = topo.mask(core, legs[0][0])
         if off and own_leaves:
             pool = _bits(full & ~off)
@@ -89,30 +106,30 @@ def _masks(topo, core, own, fwd):
             pool = _bits(full)[0::2]
         else:
             pool = _bits(full)
-        return tile, part, [(_join(pool[k::len(legs)]), leg) for k, leg in enumerate(legs)]
+        return tile, run, part, [(_join(pool[i::len(legs)]), leg) for i, leg in enumerate(legs)]
     return [with_masks(c) for c in own], [with_masks(c) for c in fwd]
 
 
-def _piece(T, tile, part, n):
+def _piece(T, tile, part, a, b):
     if part == "c":
-        return T["q%d" % tile][:, 0:n].bitcast(dt.uint8)
-    return T["p%d" % tile][:, 0:n]
+        return T["q%d" % tile][:, a:b].bitcast(dt.uint8)
+    return T["p%d" % tile][:, a:b]
 
 
-def _send(g, T, topo, call):
-    tile, part, legs = call
-    n = T.tables["WID"][tile]
-    sem = T.sem["a%s%d" % (part, tile)]
+def _send(g, T, topo, cuts, whole, call):
+    tile, run, part, legs = call
+    a, b = (0, cuts[tile][-1][1]) if part == "p" and whole[tile] else cuts[tile][run]
+    sem = T.sem["a%s%d_%d" % (part, tile, run)]
     if len(legs) == 1 and len(legs[0][1]) == 1:
         mask, (dst,) = legs[0]
         rid, pid, _ = topo.addr(dst)
-        g.remote_dma(out_ap=_piece(T, tile, part, n), in_ap=_piece(T, tile, part, n), remote_sem=sem,
+        g.remote_dma(out_ap=_piece(T, tile, part, a, b), in_ap=_piece(T, tile, part, a, b), remote_sem=sem,
                      local_sem=T.sem.sent, pid=pid, routing_id=rid, dma_engine_mask=mask)
     else:
         g.remote_dma_fused(
             [RemoteDMATransfer(dst_ids=[DstId(rid=topo.addr(d)[0], pnc=topo.addr(d)[1]) for d in dsts],
                                dma_engine_mask=mask, remote_sem=sem,
-                               srcs=[_piece(T, tile, part, n)], dsts=[_piece(T, tile, part, n) for d in dsts])
+                               srcs=[_piece(T, tile, part, a, b)], dsts=[_piece(T, tile, part, a, b) for d in dsts])
              for mask, dsts in legs],
             local_sem=T.sem.sent)
     return sum(len(_bits(mask)) for mask, dsts in legs)
@@ -124,53 +141,63 @@ def rank_program(g, core, T, topo):
         return
     cores = list(T.cores)
     seq, wid = T.tables["SEQ"], T.tables["WID"]
-    own, fwd = _routes(T, topo)
+    cuts, whole = _cuts(T, topo)
+    own, fwd = _routes(T, topo, cuts, whole)
     calls = {c: _masks(topo, c, own[c], fwd[c]) for c in cores}
     lands = {}
     for c in cores:
-        for tile, part, legs in calls[c][0] + calls[c][1]:
+        for tile, run, part, legs in calls[c][0] + calls[c][1]:
             for mask, dsts in legs:
                 if core in dsts:
-                    lands[(tile, part)] = (len(_bits(mask)), c)
+                    lands[(tile, run, part)] = (len(_bits(mask)), c)
+    dmaq = [g.sync, g.scalar]
 
-    n = wid[rank]
-    g.sync.dma_start(T.xb[:, 0:4 * n], T.x[:, 0:4 * n]).then_inc(T.sem.xl, 16)
+    for k, (a, b) in enumerate(cuts[rank]):
+        dmaq[k].dma_start(T.xb[:, 4 * a:4 * b], T.x[:, 4 * a:4 * b]).then_inc(T.sem["xl%d" % k], 16)
     g.sync.dma_start(T.wb[:], T.w[:]).then_inc(T.sem.wl, 16)
-    g.vector.wait_ge(T.sem.xl, 16)
-    g.vector.quantize_mx(T["q%d" % rank][:, 0:n], T["p%d" % rank][:, 0:n], T.xb[:, 0:4 * n]).then_inc(T.sem.qx, 1)
+    for k, (a, b) in enumerate(cuts[rank]):
+        g.vector.wait_ge(T.sem["xl%d" % k], 16)
+        g.vector.quantize_mx(T["q%d" % rank][:, a:b], T["p%d" % rank][:, a:b],
+                             T.xb[:, 4 * a:4 * b]).then_inc(T.sem["qx%d" % k], 1)
     g.vector.wait_ge(T.sem.wl, 16)
     g.vector.quantize_mx(T.qw[:], T.pw[:], T.wb[:]).then_inc(T.sem.qwd, 1)
 
     sent = 0
-    g.wait_ge(T.sem.qx, 1)
+    packed = -1
     for call in calls[core][0]:
-        sent += _send(g, T, topo, call)
+        if call[1] > packed:
+            packed = call[1]
+            g.wait_ge(T.sem["qx%d" % packed], 1)
+        sent += _send(g, T, topo, cuts, whole, call)
     for call in calls[core][1]:
-        g.wait_ge(T.sem["a%s%d" % (call[1], call[0])], lands[(call[0], call[1])][0])
-        sent += _send(g, T, topo, call)
+        g.wait_ge(T.sem["a%s%d_%d" % (call[2], call[0], call[1])], lands[call[:3]][0])
+        sent += _send(g, T, topo, cuts, whole, call)
 
     members = [j for j in range(N) if seq[j] == seq[rank]]
     col = {j: sum(wid[i] for i in members if i < j) for j in members}
 
     def expected(j):
-        relayed = any(lands[(j, part)][1] != cores[j] for part in ("c", "p"))
+        relayed = any(lands[(j, 0, part)][1] != cores[j] for part in ("c", "p"))
         return (topo.chip(cores[j]) != topo.chip(core), relayed, wid[j])
     order = [rank] + sorted((j for j in members if j != rank), key=expected)
+    blocks = [(j, k) for j in order for k in range(len(cuts[j]))]
 
     g.tensor.wait_ge(T.sem.qwd, 1)
-    for k, j in enumerate(order):
-        m, a = wid[j], col[j]
+    for i, (j, k) in enumerate(blocks):
+        a, b = cuts[j][k]
+        m, y0 = b - a, col[j] + a
         if j == rank:
-            g.tensor.wait_ge(T.sem.qx, 1)
+            g.tensor.wait_ge(T.sem["qx%d" % k], 1)
         else:
-            g.tensor.wait_ge(T.sem["ac%d" % j], lands[(j, "c")][0])
-            g.tensor.wait_ge(T.sem["ap%d" % j], lands[(j, "p")][0])
-        g.tensor.matmul_mx(T.ps[:, 512 * k:512 * k + m], T.qw[:], T.pw[:], T["q%d" % j][:, 0:m], T["p%d" % j][:, 0:m],
-                           True, True).then_inc(T.sem["mm%d" % k], 1)
-        g.vector.wait_ge(T.sem["mm%d" % k], 1)
-        g.vector.tensor_copy(T.yo[:, a:a + m], T.ps[:, 512 * k:512 * k + m]).then_inc(T.sem["cp%d" % k], 1)
-        g.sync.wait_ge(T.sem["cp%d" % k], 1)
-        g.sync.dma_start(T.y[:, a:a + m], T.yo[:, a:a + m]).then_inc(T.sem.st, 16)
+            kp = 0 if whole[j] else k
+            g.tensor.wait_ge(T.sem["ac%d_%d" % (j, k)], lands[(j, k, "c")][0])
+            g.tensor.wait_ge(T.sem["ap%d_%d" % (j, kp)], lands[(j, kp, "p")][0])
+        g.tensor.matmul_mx(T.ps[:, 512 * i:512 * i + m], T.qw[:], T.pw[:], T["q%d" % j][:, a:b], T["p%d" % j][:, a:b],
+                           True, True).then_inc(T.sem["mm%d" % i], 1)
+        g.vector.wait_ge(T.sem["mm%d" % i], 1)
+        g.vector.tensor_copy(T.yo[:, y0:y0 + m], T.ps[:, 512 * i:512 * i + m]).then_inc(T.sem["cp%d" % i], 1)
+        dmaq[i % 2].wait_ge(T.sem["cp%d" % i], 1)
+        dmaq[i % 2].dma_start(T.y[:, y0:y0 + m], T.yo[:, y0:y0 + m]).then_inc(T.sem.st, 16)
 
     g.wait_ge(T.sem.sent, sent)
-    g.wait_ge(T.sem.st, 16 * len(order))
+    g.wait_ge(T.sem.st, 16 * len(blocks))

from concourse.bass import DstId, RemoteDMATransfer
from concourse.mybir import dt

N = 8
NC = 384
YC = 744
MAXB = 4
LEAST = 128

SCRATCH = {
    "xb": ("sbuf", [128, 4 * NC], "bfloat16"),
    "wb": ("sbuf", [128, 512], "bfloat16"),
    "qw": ("sbuf", [128, 128], "float8_e4m3fn_x4"),
    "pw": ("sbuf", [128, 128], "uint8"),
    "ps": ("psum", [128, 512 * MAXB], "float32"),
    "yo": ("sbuf", [128, YC], "float32"),
}
SCRATCH.update({"q%d" % j: ("sbuf", [128, NC], "float8_e4m3fn_x4") for j in range(N)})
SCRATCH.update({"p%d" % j: ("sbuf", [128, NC], "uint8") for j in range(N)})

SEMAPHORES = (["xl0", "xl1", "wl", "qx0", "qx1", "qwd", "st", "sent"]
              + ["a%s%d_%d" % (part, j, k) for part in "cp" for j in range(N) for k in range(2)]
              + ["mm%d" % k for k in range(MAXB)] + ["cp%d" % k for k in range(MAXB)])


def _bits(mask):
    return [1 << b for b in range(mask.bit_length()) if (mask >> b) & 1]


def _join(bits):
    m = 0
    for b in bits:
        m |= b
    return m


def _cuts(T, topo):
    cores, seq, wid = list(T.cores), T.tables["SEQ"], T.tables["WID"]
    cuts, whole = [], []
    for j in range(N):
        n = wid[j]
        whole.append(any(seq[d] == seq[j] and topo.chip(cores[d]) != topo.chip(cores[j]) for d in range(N)))
        if n >= 2 * LEAST:
            h = n // 4 * 2
            cuts.append([(0, h), (h, n)])
        else:
            cuts.append([(0, n)])
    return cuts, whole


def _routes(T, topo, cuts, whole):
    cores = list(T.cores)
    seq = T.tables["SEQ"]
    own = {c: [] for c in cores}
    fwd = {c: [] for c in cores}
    for j, o in enumerate(cores):
        readers = [cores[d] for d in range(N) if seq[d] == seq[j] and d != j]
        near = [d for d in readers if topo.chip(d) == topo.chip(o)]
        far = [d for d in readers if topo.chip(d) != topo.chip(o)]
        for k in range(len(cuts[j])):
            handed = False
            plane = [] if whole[j] and k + 1 < len(cuts[j]) else [0 if whole[j] else k]
            for ch in sorted({topo.chip(d) for d in far}):
                grp = [d for d in far if topo.chip(d) == ch]
                entry, rest = grp[0], grp[1:]
                if topo.may_write(o, entry):
                    own[o].append((j, k, "c", [[entry]]))
                    own[o] += [(j, kp, "p", [grp]) for kp in plane]
                else:
                    handed = True
                    gates = [c for c in cores if c != o and topo.chip(c) == topo.chip(o) and topo.may_write(c, entry)]
                    gate_p = ([c for c in gates if c in near] + gates)[0]
                    gate_c = ([c for c in gates if c not in near] + gates)[0]
                    if gate_c not in near:
                        own[o].append((j, k, "c", [[gate_c]]))
                    if gate_p not in near:
                        own[o] += [(j, kp, "p", [[gate_p]]) for kp in plane]
                    fwd[gate_c].append((j, k, "c", [[entry]]))
                    fwd[gate_p] += [(j, kp, "p", [grp]) for kp in plane]
                if rest:
                    fwd[entry].append((j, k, "c", [rest]))
            if near:
                legs = [[d] for d in sorted(near, key=lambda d: topo.die(d) == topo.die(o))]
                for part in ("p", "c") if handed else ("c", "p"):
                    own[o] += [(j, kk, part, legs) for kk in ([k] if part == "c" else plane)]
    return own, fwd


def _masks(topo, core, own, fwd):
    def leaves(call):
        return any(topo.chip(d) != topo.chip(core) for leg in call[3] for d in leg)
    away = [d for call in own + fwd for leg in call[3] for d in leg if topo.chip(d) != topo.chip(core)]
    off = topo.mask(core, away[0]) if away else 0
    own_leaves = any(leaves(call) for call in own)

    def with_masks(call):
        tile, run, part, legs = call
        if leaves(call):
            return tile, run, part, [(topo.mask(core, leg[0]), leg) for leg in legs]
        full = topo.mask(core, legs[0][0])
        if off and own_leaves:
            pool = _bits(full & ~off)
        elif off:
            pool = _bits(full & off)
        elif len(legs) == 1:
            pool = _bits(full)[0::2]
        else:
            pool = _bits(full)
        return tile, run, part, [(_join(pool[i::len(legs)]), leg) for i, leg in enumerate(legs)]
    return [with_masks(c) for c in own], [with_masks(c) for c in fwd]


def _piece(T, tile, part, a, b):
    if part == "c":
        return T["q%d" % tile][:, a:b].bitcast(dt.uint8)
    return T["p%d" % tile][:, a:b]


def _send(g, T, topo, cuts, whole, call):
    tile, run, part, legs = call
    a, b = (0, cuts[tile][-1][1]) if part == "p" and whole[tile] else cuts[tile][run]
    sem = T.sem["a%s%d_%d" % (part, tile, run)]
    if len(legs) == 1 and len(legs[0][1]) == 1:
        mask, (dst,) = legs[0]
        rid, pid, _ = topo.addr(dst)
        g.remote_dma(out_ap=_piece(T, tile, part, a, b), in_ap=_piece(T, tile, part, a, b), remote_sem=sem,
                     local_sem=T.sem.sent, pid=pid, routing_id=rid, dma_engine_mask=mask)
    else:
        g.remote_dma_fused(
            [RemoteDMATransfer(dst_ids=[DstId(rid=topo.addr(d)[0], pnc=topo.addr(d)[1]) for d in dsts],
                               dma_engine_mask=mask, remote_sem=sem,
                               srcs=[_piece(T, tile, part, a, b)], dsts=[_piece(T, tile, part, a, b) for d in dsts])
             for mask, dsts in legs],
            local_sem=T.sem.sent)
    return sum(len(_bits(mask)) for mask, dsts in legs)


def rank_program(g, core, T, topo):
    rank = T.rank_of(core)
    if rank is None:
        return
    cores = list(T.cores)
    seq, wid = T.tables["SEQ"], T.tables["WID"]
    cuts, whole = _cuts(T, topo)
    own, fwd = _routes(T, topo, cuts, whole)
    calls = {c: _masks(topo, c, own[c], fwd[c]) for c in cores}
    lands = {}
    for c in cores:
        for tile, run, part, legs in calls[c][0] + calls[c][1]:
            for mask, dsts in legs:
                if core in dsts:
                    lands[(tile, run, part)] = (len(_bits(mask)), c)
    dmaq = [g.sync, g.scalar]

    for k, (a, b) in enumerate(cuts[rank]):
        dmaq[k].dma_start(T.xb[:, 4 * a:4 * b], T.x[:, 4 * a:4 * b]).then_inc(T.sem["xl%d" % k], 16)
    g.sync.dma_start(T.wb[:], T.w[:]).then_inc(T.sem.wl, 16)
    for k, (a, b) in enumerate(cuts[rank]):
        g.vector.wait_ge(T.sem["xl%d" % k], 16)
        g.vector.quantize_mx(T["q%d" % rank][:, a:b], T["p%d" % rank][:, a:b],
                             T.xb[:, 4 * a:4 * b]).then_inc(T.sem["qx%d" % k], 1)
    g.vector.wait_ge(T.sem.wl, 16)
    g.vector.quantize_mx(T.qw[:], T.pw[:], T.wb[:]).then_inc(T.sem.qwd, 1)

    sent = 0
    packed = -1
    for call in calls[core][0]:
        if call[1] > packed:
            packed = call[1]
            g.wait_ge(T.sem["qx%d" % packed], 1)
        sent += _send(g, T, topo, cuts, whole, call)
    for call in calls[core][1]:
        g.wait_ge(T.sem["a%s%d_%d" % (call[2], call[0], call[1])], lands[call[:3]][0])
        sent += _send(g, T, topo, cuts, whole, call)

    members = [j for j in range(N) if seq[j] == seq[rank]]
    col = {j: sum(wid[i] for i in members if i < j) for j in members}

    def expected(j):
        relayed = any(lands[(j, 0, part)][1] != cores[j] for part in ("c", "p"))
        return (topo.chip(cores[j]) != topo.chip(core), relayed, wid[j])
    order = [rank] + sorted((j for j in members if j != rank), key=expected)
    blocks = [(j, k) for j in order for k in range(len(cuts[j]))]

    g.tensor.wait_ge(T.sem.qwd, 1)
    for i, (j, k) in enumerate(blocks):
        a, b = cuts[j][k]
        m, y0 = b - a, col[j] + a
        if j == rank:
            g.tensor.wait_ge(T.sem["qx%d" % k], 1)
        else:
            kp = 0 if whole[j] else k
            g.tensor.wait_ge(T.sem["ac%d_%d" % (j, k)], lands[(j, k, "c")][0])
            g.tensor.wait_ge(T.sem["ap%d_%d" % (j, kp)], lands[(j, kp, "p")][0])
        g.tensor.matmul_mx(T.ps[:, 512 * i:512 * i + m], T.qw[:], T.pw[:], T["q%d" % j][:, a:b], T["p%d" % j][:, a:b],
                           True, True).then_inc(T.sem["mm%d" % i], 1)
        g.vector.wait_ge(T.sem["mm%d" % i], 1)
        g.vector.tensor_copy(T.yo[:, y0:y0 + m], T.ps[:, 512 * i:512 * i + m]).then_inc(T.sem["cp%d" % i], 1)
        dmaq[i % 2].wait_ge(T.sem["cp%d" % i], 1)
        dmaq[i % 2].dma_start(T.y[:, y0:y0 + m], T.yo[:, y0:y0 + m]).then_inc(T.sem.st, 16)

    g.wait_ge(T.sem.sent, sent)
    g.wait_ge(T.sem.st, 16 * len(blocks))
